import numpy as np
import ml_dtypes


def mxq(x, axis, fmt="e4m3"):
    dtype, down = {"e4m3": (ml_dtypes.float8_e4m3fn, 7), "e5m2": (ml_dtypes.float8_e5m2, 14)}[fmt]
    v = np.moveaxis(np.asarray(x, np.float32).astype(ml_dtypes.bfloat16).astype(np.float64), axis, -1)
    blocks = v.reshape(v.shape[:-1] + (-1, 32))
    amax = np.abs(blocks).max(-1, keepdims=True)
    byte = np.maximum(np.where(amax > 0, np.frexp(amax)[1] - 1 + 127, 0) - down, 1)
    scale = np.exp2(byte - 127.0)
    codes = (blocks / scale).astype(np.float32).astype(dtype).astype(np.float64)
    return np.moveaxis((codes * scale).reshape(v.shape), -1, axis)


WIDE = False


def mx_kscale(k):
    if not WIDE:
        return np.ones(k)
    levels = np.array([10, -10, 5, -5, 0])
    if k % 512:
        return np.exp2(np.random.permutation(np.resize(levels, k // 32))).repeat(32)
    a = np.empty((k // 512, 16))
    for p in range(k // 512):
        a[p, :8] = np.random.permutation(np.resize(levels, 8))
        for g in range(8):
            far = levels[np.abs(levels - a[p, g]) >= 10]
            a[p, g + 8] = far[np.random.randint(len(far))]
    return np.exp2(a.ravel()).repeat(32)


def f64(x):
    return np.asarray(x).astype(np.float64)


def striped(idx):
    return np.tile(idx.reshape(-1, 16).T, (8, 1)).astype(np.uint16)


def unstriped(offs):
    return offs[:16].T.reshape(-1).astype(np.int64)


def striped8(idx):
    return np.concatenate([x.reshape(-1, 16).T for x in idx]).astype(np.uint16)


def runs(offs, k):
    lists = np.stack([offs[16 * r : 16 * r + 16].T.reshape(-1) for r in range(8)]).astype(np.int64)
    return lists[np.arange(k) % 512 // 64]


def pack_weight(w):
    k, n = w.shape
    w = f64(np.asarray(w, np.float32).astype(ml_dtypes.bfloat16)).reshape(k // 32, 32, n)
    amax = np.abs(w).max(1)
    byte = np.clip(np.where(amax > 0, np.frexp(amax)[1] - 1 + 127 - 7, 1), 1, 254)
    scaled = (w * np.exp2(127.0 - byte)[:, None, :]).reshape(k, n).astype(np.float32)
    words = np.ascontiguousarray(scaled.reshape(k // 512, 128, 4, n).transpose(0, 1, 3, 2)).astype(ml_dtypes.float8_e4m3fn).view(np.uint8)
    return words, np.ascontiguousarray(byte.astype(np.uint8).reshape(k // 512, 16, n))


def unpack_weight(words, scales):
    g, p, n, _ = words.shape
    vals = np.ascontiguousarray(words).view(ml_dtypes.float8_e4m3fn).astype(np.float64) * np.repeat(np.exp2(scales.astype(np.float64) - 127.0), 8, axis=1)[..., None]
    return vals.transpose(0, 1, 3, 2).reshape(g * 512, n)


K, T, S, N, G, H = 512, 2048, 512, 512, 2048, 512


def setup_inputs():
    n = np.random.standard_normal
    s = mx_kscale(K)[:, None]
    u = mx_kscale(S)
    packed_xT = pack_weight(n((K, T)) * s)
    packed_dT = pack_weight(n((K, G)) / s)
    return {
        "x_words": packed_xT[0],
        "x_scales": packed_xT[1],
        "d_words": packed_dT[0],
        "d_scales": packed_dT[1],
        "gn": (np.random.uniform(0.5, 1.5, (H, 1)) * u[:, None]).astype(np.float32),
        "w1": (n((H, N)) / np.sqrt(2 * H) / u[:, None]).astype(np.float32),
        "w2": (n((K, N)) / np.sqrt(2 * K) / s).astype(np.float32),
        "offs": striped(np.random.permutation(T)[:S]),
        "k1": striped8(np.random.randint(0, G, (8, H))),
        "n1": striped(np.random.permutation(S)),
        "n2": striped(np.random.permutation(S)),
        "two": striped(np.random.permutation(T)[:S]),
        "n3": striped(np.random.permutation(S)),
        "n4": striped(np.random.permutation(S)),
    }


def reference(x_words, x_scales, d_words, d_scales, gn, w1, w2, offs, k1, n1, n2, two, n3, n4):
    d_k1 = unpack_weight(d_words, d_scales)[np.arange(K)[:, None], runs(k1, K)]
    xq = unpack_weight(x_words, x_scales)[:, unstriped(offs)]
    s = 0.0625 * (d_k1.T @ xq)
    ex = np.exp(s)
    z = f64(gn) * (np.log(ex + ex[:, unstriped(n1)]) - s[:, unstriped(n2)])
    x_two = unpack_weight(x_words, x_scales)[:, unstriped(two)]
    h = mxq(f64(w1), 0, "e4m3").T @ mxq(z, 0, "e4m3") + mxq(f64(w2), 0, "e4m3").T @ x_two
    st = h + 0.5 * h[:, unstriped(n3)]
    return st - st[:, unstriped(n4)]

@@ -1,0 +1,207 @@
+from contextlib import ExitStack
+
+import concourse.mybir as mybir
+
+K, T, S, N, G, H = 512, 2048, 512, 512, 2048, 512
+FLOPS = 3 * 2 * 512 * 512 * 512
+
+F32 = mybir.dt.float32
+BF16 = mybir.dt.bfloat16
+I32 = mybir.dt.int32
+U32 = mybir.dt.uint32
+U16 = mybir.dt.uint16
+U8 = mybir.dt.uint8
+FP8X4 = mybir.dt.float8_e4m3fn_x4
+ACT = mybir.ActivationFunctionType
+ALU = mybir.AluOpType
+
+P = 128
+PACK = 4
+HALF = S // 2
+HALF_COLS = HALF // 16
+
+
+def tile_picked_kmixlsehop_none_p_kernel(tc, x_words, x_scales, d_words, d_scales, gn, w1, w2, offs, k1, n1, n2, two, n3, n4, out):
+    nc = tc.nc
+    with ExitStack() as ctx:
+        lists = ctx.enter_context(tc.tile_pool(name="lists", bufs=1))
+        keep = ctx.enter_context(tc.tile_pool(name="keep", bufs=1))
+        psum = ctx.enter_context(tc.psum_pool(name="psum", bufs=1))
+
+        def load_list(src, name):
+            t = lists.tile([P, S // 16], U16, name=name)
+            nc.sync.dma_start(t[:], src)
+            return t
+
+        def half(a):
+            return slice(a * HALF, (a + 1) * HALF)
+
+        def half_list(lst, a):
+            return lst[:, a * HALF_COLS : (a + 1) * HALF_COLS]
+
+        d_scale_table = keep.tile([P, G], U8, name="d_scale_table", align_bytes=64)
+        x_scale_table = keep.tile([P, T], U8, name="x_scale_table", align_bytes=64)
+        nc.gpsimd.memset(x_scale_table[:].bitcast(I32), 0)
+        x_rows = x_scales[0].bitcast(I32).rearrange("(q r) c -> r q c", r=4)
+        for r in range(4):
+            nc.gpsimd.dma_start(x_scale_table[r:P:32, :].bitcast(I32), x_rows[r])
+        gain = keep.tile([P, PACK], F32, name="gain")
+        nc.gpsimd.dma_start(gain[:], gn.rearrange("(p t) o -> p (t o)", t=PACK))
+
+        k1_t = load_list(k1, "k1_t")
+        d_rows = d_scales[0].bitcast(I32).rearrange("(g r) c -> r g c", r=2)
+        for r in range(2):
+            nc.sync.dma_start(
+                d_scale_table[r:P:2, :].bitcast(I32),
+                d_rows[r].unsqueeze(1).to_broadcast([8, 8, G // 4]),
+            )
+        offs_t = load_list(offs, "offs_t")
+        two_t = load_list(two, "two_t")
+        w2_raw = keep.tile([P, PACK, N], F32, name="w2_raw", tag="w_raw")
+        nc.sync.dma_start(w2_raw[:], w2.rearrange("(p j) n -> p j n", j=PACK))
+        d_table = keep.tile([P, G], U32, name="d_table", align_bytes=64)
+        nc.sync.dma_start(d_table[:].bitcast(I32), d_words[0].rearrange("p n t -> p (n t)").bitcast(I32))
+        x_table = keep.tile([P, T], U32, name="x_table", align_bytes=64)
+        nc.sync.dma_start(x_table[:].bitcast(I32), x_words[0].rearrange("p n t -> p (n t)").bitcast(I32))
+        n1_t = load_list(n1, "n1_t")
+        n2_t = load_list(n2, "n2_t")
+        n3_t = load_list(n3, "n3_t")
+        n4_t = load_list(n4, "n4_t")
+
+        key_scales_picked = keep.tile([P, H], U8, name="key_scales_picked", align_bytes=64)
+        nc.vector.tensor_copy(key_scales_picked[:], d_scale_table[:].indirect(k1_t[:]))
+        key_scales = keep.tile([P, H], U8, name="key_scales", align_bytes=64)
+        nc.vector.tensor_copy(
+            key_scales[:].rearrange("p (t m) -> p m t", t=PACK),
+            key_scales_picked[:].rearrange("p (m t) -> p m t", t=PACK),
+        )
+        for r in range(2):
+            nc.scalar.dma_start(key_scales[2 + r : P : 32, :].bitcast(I32), key_scales[16 + r : P : 32, :].bitcast(I32))
+
+        q_scales = keep.tile([P, S], U8, name="q_scales", align_bytes=64)
+        nc.vector.tensor_copy(q_scales[:], x_scale_table[:].indirect(offs_t[:]))
+        two_scales = keep.tile([P, S], U8, name="two_scales", align_bytes=64)
+        nc.vector.tensor_copy(two_scales[:], x_scale_table[:].indirect(two_t[:]))
+
+        def interleave(eng_copy, dst, src):
+            eng_copy(
+                dst[:].rearrange("p (c i) t -> p c t i", i=4),
+                src[:].rearrange("p t (c i) -> p c t i", i=4),
+            )
+
+        def quantize(src, width, name):
+            codes = keep.tile([P, width], U32, name=name + "_codes", align_bytes=64)
+            scales = keep.tile([P, width], U8, name=name + "_scales", align_bytes=64)
+            nc.vector.quantize_mx(out=codes[:].bitcast(FP8X4), scales=scales[:], in_=src[:].rearrange("p n t -> p (n t)"))
+            return codes, scales
+
+        w2_bf = keep.tile([P, N, PACK], BF16, name="w2_bf", align_bytes=64)
+        interleave(nc.scalar.copy, w2_bf, w2_raw)
+        w1_raw = keep.tile([P, PACK, N], F32, name="w1_raw", tag="w_raw")
+        nc.sync.dma_start(w1_raw[:], w1.rearrange("(p j) n -> p j n", j=PACK))
+
+        key_words_picked = keep.tile([P, H], U32, name="key_words_picked", align_bytes=64)
+        nc.vector.tensor_copy(key_words_picked[:], d_table[:].indirect(k1_t[:]))
+        key_words = keep.tile([P, H], U32, name="key_words", align_bytes=64)
+        nc.vector.tensor_copy(
+            key_words[:].rearrange("p (t m) -> p m t", t=PACK),
+            key_words_picked[:].rearrange("p (m t) -> p m t", t=PACK),
+        )
+        q_words = keep.tile([P, S], U32, name="q_words", align_bytes=64)
+        nc.vector.tensor_copy(q_words[:], x_table[:].indirect(offs_t[:]))
+
+        score_ps = []
+        for t in range(PACK):
+            ps = psum.tile([P, S], F32, name="score%d" % t, tag="bank%d" % t)
+            cols = slice(t * P, (t + 1) * P)
+            nc.tensor.matmul_mx(
+                out=ps[:],
+                lhsT=key_words[:, cols].bitcast(FP8X4),
+                lhsT_scale=key_scales[:, cols],
+                rhs=q_words[:].bitcast(FP8X4),
+                rhs_scale=q_scales[:],
+                start=True,
+                stop=True,
+            )
+            score_ps.append(ps)
+
+        ex = []
+        for t in range(PACK):
+            e = keep.tile([P, S], F32, name="ex%d" % t)
+            nc.scalar.activation(e[:], score_ps[t][:], ACT.Exp, scale=0.0625)
+            ex.append(e)
+
+        two_words = keep.tile([P, S], U32, name="two_words", align_bytes=64)
+        nc.vector.tensor_copy(two_words[:], x_table[:].indirect(two_t[:]))
+        neg_gain = keep.tile([P, PACK], F32, name="neg_gain")
+        nc.vector.tensor_scalar(neg_gain[:], gain[:], -0.0625, None, ALU.mult)
+
+        total = []
+        scaled = []
+        for t in range(PACK):
+            twin = keep.tile([P, S], F32, name="ex_twin%d" % t)
+            nc.vector.tensor_copy(twin[:], ex[t][:])
+            tot = keep.tile([P, S], F32, name="total%d" % t)
+            for a in range(2):
+                nc.vector.tensor_tensor(tot[:, half(a)], ex[t][:].indirect(half_list(n1_t, a)), twin[:, half(a)], ALU.add)
+            total.append(tot)
+            sc = keep.tile([P, S], F32, name="scaled%d" % t)
+            nc.scalar.activation(sc[:], score_ps[t][:], ACT.Copy, scale=neg_gain[:, t : t + 1])
+            scaled.append(sc)
+
+        w2_codes, w2_scales = quantize(w2_bf, N, "w2")
+        w1_bf = keep.tile([P, N, PACK], BF16, name="w1_bf", align_bytes=64)
+        interleave(nc.vector.tensor_copy, w1_bf, w1_raw)
+        w1_codes, w1_scales = quantize(w1_bf, N, "w1")
+
+        h = [keep.tile([P, S], F32, name="h%d" % m) for m in range(PACK)]
+        for a in range(2):
+            z_planes = keep.tile([P, PACK, HALF], BF16, name="z_planes%d" % a)
+            for t in range(PACK):
+                picked = keep.tile([P, HALF], F32, name="picked%d_%d" % (a, t))
+                nc.scalar.activation(picked[:], scaled[t][:].indirect(half_list(n2_t, a)), ACT.Copy)
+                lse = keep.tile([P, HALF], F32, name="lse%d_%d" % (a, t))
+                nc.scalar.activation(lse[:], total[t][:, half(a)], ACT.Ln)
+                nc.vector.scalar_tensor_tensor(z_planes[:, t, :], lse[:], gain[:, t : t + 1], picked[:], ALU.mult, ALU.add)
+            z_bf = keep.tile([P, HALF, PACK], BF16, name="z_bf%d" % a, align_bytes=64)
+            interleave(nc.vector.tensor_copy, z_bf, z_planes)
+            z_codes, z_scales = quantize(z_bf, HALF, "z%d" % a)
+            for m in range(PACK):
+                ps = psum.tile([P, HALF], F32, name="h_ps%d_%d" % (a, m), tag="bank%d" % (PACK * (1 - a) + m))
+                cols = slice(m * P, (m + 1) * P)
+                nc.tensor.matmul_mx(
+                    out=ps[:],
+                    lhsT=w2_codes[:, cols].bitcast(FP8X4),
+                    lhsT_scale=w2_scales[:, cols],
+                    rhs=two_words[:, half(a)].bitcast(FP8X4),
+                    rhs_scale=two_scales[:, half(a)],
+                    start=True,
+                    stop=False,
+                )
+                nc.tensor.matmul_mx(
+                    out=ps[:],
+                    lhsT=w1_codes[:, cols].bitcast(FP8X4),
+                    lhsT_scale=w1_scales[:, cols],
+                    rhs=z_codes[:].bitcast(FP8X4),
+                    rhs_scale=z_scales[:],
+                    start=False,
+                    stop=True,
+                )
+                nc.scalar.copy(h[m][:, half(a)], ps[:])
+
+        for m in range(PACK):
+            neg_st = keep.tile([P, S], F32, name="neg_st%d" % m)
+            for a in range(2):
+                hop = keep.tile([P, HALF], F32, name="hop%d_%d" % (m, a))
+                nc.scalar.activation(hop[:], h[m][:].indirect(half_list(n3_t, a)), ACT.Copy, scale=-0.5)
+                nc.vector.tensor_tensor(neg_st[:, half(a)], hop[:], h[m][:, half(a)], ALU.subtract)
+            res = keep.tile([P, S], F32, name="res%d" % m)
+            for a in range(2):
+                other = keep.tile([P, HALF], F32, name="other%d_%d" % (m, a))
+                if a == 0 or m == 0:
+                    nc.vector.tensor_copy(other[:], neg_st[:, half(a)])
+                    nc.vector.tensor_tensor(res[:, half(a)], neg_st[:].indirect(half_list(n4_t, a)), other[:], ALU.subtract)
+                else:
+                    nc.scalar.activation(other[:], neg_st[:].indirect(half_list(n4_t, a)), ACT.Copy)
+                    nc.vector.tensor_tensor(res[:, half(a)], other[:], neg_st[:, half(a)], ALU.subtract)
+            nc.sync.dma_start(out[m * P : (m + 1) * P, :], res[:])

@@ -41,30 +41,28 @@ def tile_picked_kmixlsehop_none_p_kernel(tc, x_words, x_scales, d_words, d_scale
 
         d_scale_table = keep.tile([P, G], U8, name="d_scale_table", align_bytes=64)
         x_scale_table = keep.tile([P, T], U8, name="x_scale_table", align_bytes=64)
-        nc.gpsimd.memset(x_scale_table[:].bitcast(I32), 0)
-        x_rows = x_scales[0].bitcast(I32).rearrange("(q r) c -> r q c", r=4)
-        for r in range(4):
-            nc.gpsimd.dma_start(x_scale_table[r:P:32, :].bitcast(I32), x_rows[r])
+        nc.vector.memset(x_scale_table[:].bitcast(I32), 0)
         gain = keep.tile([P, PACK], F32, name="gain")
         nc.gpsimd.dma_start(gain[:], gn.rearrange("(p t) o -> p (t o)", t=PACK))
 
         k1_t = load_list(k1, "k1_t")
-        d_rows = d_scales[0].bitcast(I32).rearrange("(g r) c -> r g c", r=2)
-        for r in range(2):
-            nc.sync.dma_start(
-                d_scale_table[r:P:2, :].bitcast(I32),
-                d_rows[r].unsqueeze(1).to_broadcast([8, 8, G // 4]),
-            )
+        nc.sync.dma_start(
+            d_scale_table[:].bitcast(I32),
+            d_scales[0].bitcast(I32).unsqueeze(1).to_broadcast([16, 8, G // 4]),
+        )
         offs_t = load_list(offs, "offs_t")
-        two_t = load_list(two, "two_t")
-        w2_raw = keep.tile([P, PACK, N], F32, name="w2_raw", tag="w_raw")
-        nc.sync.dma_start(w2_raw[:], w2.rearrange("(p j) n -> p j n", j=PACK))
-        d_table = keep.tile([P, G], U32, name="d_table", align_bytes=64)
-        nc.sync.dma_start(d_table[:].bitcast(I32), d_words[0].rearrange("p n t -> p (n t)").bitcast(I32))
+        x_rows = x_scales[0].bitcast(I32).rearrange("(q r) c -> r q c", r=4)
+        for r in range(4):
+            nc.scalar.dma_start(x_scale_table[r:P:32, :].bitcast(I32), x_rows[r])
         x_table = keep.tile([P, T], U32, name="x_table", align_bytes=64)
         nc.sync.dma_start(x_table[:].bitcast(I32), x_words[0].rearrange("p n t -> p (n t)").bitcast(I32))
+        d_table = keep.tile([P, G], U32, name="d_table", align_bytes=64)
+        nc.sync.dma_start(d_table[:].bitcast(I32), d_words[0].rearrange("p n t -> p (n t)").bitcast(I32))
+        two_t = load_list(two, "two_t")
         n1_t = load_list(n1, "n1_t")
         n2_t = load_list(n2, "n2_t")
+        w2_raw = keep.tile([P, PACK, N], F32, name="w2_raw", tag="w_raw")
+        nc.sync.dma_start(w2_raw[:], w2.rearrange("(p j) n -> p j n", j=PACK))
         n3_t = load_list(n3, "n3_t")
         n4_t = load_list(n4, "n4_t")
 
@@ -75,13 +73,8 @@ def tile_picked_kmixlsehop_none_p_kernel(tc, x_words, x_scales, d_words, d_scale
             key_scales[:].rearrange("p (t m) -> p m t", t=PACK),
             key_scales_picked[:].rearrange("p (m t) -> p m t", t=PACK),
         )
-        for r in range(2):
-            nc.scalar.dma_start(key_scales[2 + r : P : 32, :].bitcast(I32), key_scales[16 + r : P : 32, :].bitcast(I32))
-
-        q_scales = keep.tile([P, S], U8, name="q_scales", align_bytes=64)
-        nc.vector.tensor_copy(q_scales[:], x_scale_table[:].indirect(offs_t[:]))
-        two_scales = keep.tile([P, S], U8, name="two_scales", align_bytes=64)
-        nc.vector.tensor_copy(two_scales[:], x_scale_table[:].indirect(two_t[:]))
+        for r in range(1, 4):
+            nc.scalar.dma_start(key_scales[r:P:32, :].bitcast(I32), key_scales[8 * r : P : 32, :].bitcast(I32))
 
         def interleave(eng_copy, dst, src):
             eng_copy(
@@ -95,29 +88,22 @@ def tile_picked_kmixlsehop_none_p_kernel(tc, x_words, x_scales, d_words, d_scale
             nc.vector.quantize_mx(out=codes[:].bitcast(FP8X4), scales=scales[:], in_=src[:].rearrange("p n t -> p (n t)"))
             return codes, scales
 
-        w2_bf = keep.tile([P, N, PACK], BF16, name="w2_bf", align_bytes=64)
-        interleave(nc.scalar.copy, w2_bf, w2_raw)
-        w1_raw = keep.tile([P, PACK, N], F32, name="w1_raw", tag="w_raw")
-        nc.sync.dma_start(w1_raw[:], w1.rearrange("(p j) n -> p j n", j=PACK))
-
-        key_words_picked = keep.tile([P, H], U32, name="key_words_picked", align_bytes=64)
-        nc.vector.tensor_copy(key_words_picked[:], d_table[:].indirect(k1_t[:]))
-        key_words = keep.tile([P, H], U32, name="key_words", align_bytes=64)
-        nc.vector.tensor_copy(
-            key_words[:].rearrange("p (t m) -> p m t", t=PACK),
-            key_words_picked[:].rearrange("p (m t) -> p m t", t=PACK),
-        )
+        q_scales = keep.tile([P, S], U8, name="q_scales", align_bytes=64)
+        nc.vector.tensor_copy(q_scales[:], x_scale_table[:].indirect(offs_t[:]))
         q_words = keep.tile([P, S], U32, name="q_words", align_bytes=64)
         nc.vector.tensor_copy(q_words[:], x_table[:].indirect(offs_t[:]))
+        key_words_picked = keep.tile([P, H], U32, name="key_words_picked", align_bytes=64)
+        nc.vector.tensor_copy(key_words_picked[:], d_table[:].indirect(k1_t[:]))
 
         score_ps = []
         for t in range(PACK):
+            key_words = keep.tile([P, P], U32, name="key_words%d" % t, align_bytes=64)
+            nc.vector.tensor_copy(key_words[:], key_words_picked[:, t:H:PACK])
             ps = psum.tile([P, S], F32, name="score%d" % t, tag="bank%d" % t)
-            cols = slice(t * P, (t + 1) * P)
             nc.tensor.matmul_mx(
                 out=ps[:],
-                lhsT=key_words[:, cols].bitcast(FP8X4),
-                lhsT_scale=key_scales[:, cols],
+                lhsT=key_words[:].bitcast(FP8X4),
+                lhsT_scale=key_scales[:, t * P : (t + 1) * P],
                 rhs=q_words[:].bitcast(FP8X4),
                 rhs_scale=q_scales[:],
                 start=True,
@@ -131,22 +117,27 @@ def tile_picked_kmixlsehop_none_p_kernel(tc, x_words, x_scales, d_words, d_scale
             nc.scalar.activation(e[:], score_ps[t][:], ACT.Exp, scale=0.0625)
             ex.append(e)
 
+        two_scales = keep.tile([P, S], U8, name="two_scales", align_bytes=64)
+        nc.vector.tensor_copy(two_scales[:], x_scale_table[:].indirect(two_t[:]))
         two_words = keep.tile([P, S], U32, name="two_words", align_bytes=64)
         nc.vector.tensor_copy(two_words[:], x_table[:].indirect(two_t[:]))
-        neg_gain = keep.tile([P, PACK], F32, name="neg_gain")
-        nc.vector.tensor_scalar(neg_gain[:], gain[:], -0.0625, None, ALU.mult)
+
+        w2_bf = keep.tile([P, N, PACK], BF16, name="w2_bf", align_bytes=64)
+        interleave(nc.vector.tensor_copy, w2_bf, w2_raw)
+        w1_raw = keep.tile([P, PACK, N], F32, name="w1_raw", tag="w_raw")
+        nc.sync.dma_start(w1_raw[:], w1.rearrange("(p j) n -> p j n", j=PACK))
 
         total = []
         scaled = []
         for t in range(PACK):
             twin = keep.tile([P, S], F32, name="ex_twin%d" % t)
-            nc.vector.tensor_copy(twin[:], ex[t][:])
+            nc.sync.dma_start(twin[:], ex[t][:])
             tot = keep.tile([P, S], F32, name="total%d" % t)
             for a in range(2):
                 nc.vector.tensor_tensor(tot[:, half(a)], ex[t][:].indirect(half_list(n1_t, a)), twin[:, half(a)], ALU.add)
             total.append(tot)
             sc = keep.tile([P, S], F32, name="scaled%d" % t)
-            nc.scalar.activation(sc[:], score_ps[t][:], ACT.Copy, scale=neg_gain[:, t : t + 1])
+            nc.scalar.activation(sc[:], score_ps[t][:], ACT.Copy, scale=gain[:, t : t + 1])
             scaled.append(sc)
 
         w2_codes, w2_scales = quantize(w2_bf, N, "w2")
@@ -154,12 +145,13 @@ def tile_picked_kmixlsehop_none_p_kernel(tc, x_words, x_scales, d_words, d_scale
         interleave(nc.vector.tensor_copy, w1_bf, w1_raw)
         w1_codes, w1_scales = quantize(w1_bf, N, "w1")
 
+        h_ps = {}
         h = [keep.tile([P, S], F32, name="h%d" % m) for m in range(PACK)]
         for a in range(2):
             z_planes = keep.tile([P, PACK, HALF], BF16, name="z_planes%d" % a)
             for t in range(PACK):
                 picked = keep.tile([P, HALF], F32, name="picked%d_%d" % (a, t))
-                nc.scalar.activation(picked[:], scaled[t][:].indirect(half_list(n2_t, a)), ACT.Copy)
+                nc.scalar.activation(picked[:], scaled[t][:].indirect(half_list(n2_t, a)), ACT.Copy, scale=-0.0625)
                 lse = keep.tile([P, HALF], F32, name="lse%d_%d" % (a, t))
                 nc.scalar.activation(lse[:], total[t][:, half(a)], ACT.Ln)
                 nc.vector.scalar_tensor_tensor(z_planes[:, t, :], lse[:], gain[:, t : t + 1], picked[:], ALU.mult, ALU.add)
@@ -187,14 +179,21 @@ def tile_picked_kmixlsehop_none_p_kernel(tc, x_words, x_scales, d_words, d_scale
                     start=False,
                     stop=True,
                 )
-                nc.scalar.copy(h[m][:, half(a)], ps[:])
+                h_ps[a, m] = ps
+                if a == 0:
+                    nc.scalar.copy(h[m][:, half(a)], ps[:])
 
         for m in range(PACK):
+            nc.scalar.copy(h[m][:, half(1)], h_ps[1, m][:])
             neg_st = keep.tile([P, S], F32, name="neg_st%d" % m)
-            for a in range(2):
+            for a in (1, 0):
                 hop = keep.tile([P, HALF], F32, name="hop%d_%d" % (m, a))
-                nc.scalar.activation(hop[:], h[m][:].indirect(half_list(n3_t, a)), ACT.Copy, scale=-0.5)
-                nc.vector.tensor_tensor(neg_st[:, half(a)], hop[:], h[m][:, half(a)], ALU.subtract)
+                if m == 0 and a == 1:
+                    nc.vector.tensor_copy(hop[:], h[m][:].indirect(half_list(n3_t, a)))
+                    nc.vector.scalar_tensor_tensor(neg_st[:, half(a)], hop[:], -0.5, h[m][:, half(a)], ALU.mult, ALU.subtract)
+                else:
+                    nc.scalar.activation(hop[:], h[m][:].indirect(half_list(n3_t, a)), ACT.Copy, scale=-0.5)
+                    nc.vector.tensor_tensor(neg_st[:, half(a)], hop[:], h[m][:, half(a)], ALU.subtract)
             res = keep.tile([P, S], F32, name="res%d" % m)
             for a in range(2):
                 other = keep.tile([P, HALF], F32, name="other%d_%d" % (m, a))

@@ -17,6 +17,7 @@ ALU = mybir.AluOpType
 
 P = 128
 PACK = 4
+RUN = 8
 HALF = S // 2
 HALF_COLS = HALF // 16
 
@@ -42,8 +43,10 @@ def tile_picked_kmixlsehop_none_p_kernel(tc, x_words, x_scales, d_words, d_scale
         d_scale_table = keep.tile([P, G], U8, name="d_scale_table", align_bytes=64)
         x_scale_table = keep.tile([P, T], U8, name="x_scale_table", align_bytes=64)
         nc.vector.memset(x_scale_table[:].bitcast(I32), 0)
-        gain = keep.tile([P, PACK], F32, name="gain")
-        nc.gpsimd.dma_start(gain[:], gn.rearrange("(p t) o -> p (t o)", t=PACK))
+        gain = [keep.tile([P, 1], F32, name="gain%d" % t) for t in range(PACK)]
+        gain_rows = gn.rearrange("(b t r) o -> t b r o", t=PACK, r=RUN)
+        for t in range(PACK):
+            nc.gpsimd.dma_start(gain[t][:], gain_rows[t])
 
         k1_t = load_list(k1, "k1_t")
         nc.sync.dma_start(
@@ -54,10 +57,10 @@ def tile_picked_kmixlsehop_none_p_kernel(tc, x_words, x_scales, d_words, d_scale
         x_rows = x_scales[0].bitcast(I32).rearrange("(q r) c -> r q c", r=4)
         for r in range(4):
             nc.scalar.dma_start(x_scale_table[r:P:32, :].bitcast(I32), x_rows[r])
-        x_table = keep.tile([P, T], U32, name="x_table", align_bytes=64)
-        nc.sync.dma_start(x_table[:].bitcast(I32), x_words[0].rearrange("p n t -> p (n t)").bitcast(I32))
         d_table = keep.tile([P, G], U32, name="d_table", align_bytes=64)
         nc.sync.dma_start(d_table[:].bitcast(I32), d_words[0].rearrange("p n t -> p (n t)").bitcast(I32))
+        x_table = keep.tile([P, T], U32, name="x_table", align_bytes=64)
+        nc.sync.dma_start(x_table[:].bitcast(I32), x_words[0].rearrange("p n t -> p (n t)").bitcast(I32))
         two_t = load_list(two, "two_t")
         n1_t = load_list(n1, "n1_t")
         n2_t = load_list(n2, "n2_t")
@@ -70,8 +73,8 @@ def tile_picked_kmixlsehop_none_p_kernel(tc, x_words, x_scales, d_words, d_scale
         nc.vector.tensor_copy(key_scales_picked[:], d_scale_table[:].indirect(k1_t[:]))
         key_scales = keep.tile([P, H], U8, name="key_scales", align_bytes=64)
         nc.vector.tensor_copy(
-            key_scales[:].rearrange("p (t m) -> p m t", t=PACK),
-            key_scales_picked[:].rearrange("p (m t) -> p m t", t=PACK),
+            key_scales[:].bitcast(I32).rearrange("p (t b r) -> p t b r", t=PACK, r=RUN // 4),
+            key_scales_picked[:].bitcast(I32).rearrange("p (b t r) -> p t b r", t=PACK, r=RUN // 4),
         )
         for r in range(1, 4):
             nc.scalar.dma_start(key_scales[r:P:32, :].bitcast(I32), key_scales[8 * r : P : 32, :].bitcast(I32))
@@ -88,21 +91,24 @@ def tile_picked_kmixlsehop_none_p_kernel(tc, x_words, x_scales, d_words, d_scale
             nc.vector.quantize_mx(out=codes[:].bitcast(FP8X4), scales=scales[:], in_=src[:].rearrange("p n t -> p (n t)"))
             return codes, scales
 
+        key_words_picked = keep.tile([P, H], U32, name="key_words_picked", align_bytes=64)
+        nc.vector.tensor_copy(key_words_picked[:], d_table[:].indirect(k1_t[:]))
+        key_words = keep.tile([P, H], U32, name="key_words", align_bytes=64)
+        nc.vector.tensor_copy(
+            key_words[:].rearrange("p (t b r) -> p t b r", t=PACK, r=RUN),
+            key_words_picked[:].rearrange("p (b t r) -> p t b r", t=PACK, r=RUN),
+        )
         q_scales = keep.tile([P, S], U8, name="q_scales", align_bytes=64)
         nc.vector.tensor_copy(q_scales[:], x_scale_table[:].indirect(offs_t[:]))
         q_words = keep.tile([P, S], U32, name="q_words", align_bytes=64)
         nc.vector.tensor_copy(q_words[:], x_table[:].indirect(offs_t[:]))
-        key_words_picked = keep.tile([P, H], U32, name="key_words_picked", align_bytes=64)
-        nc.vector.tensor_copy(key_words_picked[:], d_table[:].indirect(k1_t[:]))
 
         score_ps = []
         for t in range(PACK):
-            key_words = keep.tile([P, P], U32, name="key_words%d" % t, align_bytes=64)
-            nc.vector.tensor_copy(key_words[:], key_words_picked[:, t:H:PACK])
             ps = psum.tile([P, S], F32, name="score%d" % t, tag="bank%d" % t)
             nc.tensor.matmul_mx(
                 out=ps[:],
-                lhsT=key_words[:].bitcast(FP8X4),
+                lhsT=key_words[:, t * P : (t + 1) * P].bitcast(FP8X4),
                 lhsT_scale=key_scales[:, t * P : (t + 1) * P],
                 rhs=q_words[:].bitcast(FP8X4),
                 rhs_scale=q_scales[:],
@@ -119,25 +125,29 @@ def tile_picked_kmixlsehop_none_p_kernel(tc, x_words, x_scales, d_words, d_scale
 
         two_scales = keep.tile([P, S], U8, name="two_scales", align_bytes=64)
         nc.vector.tensor_copy(two_scales[:], x_scale_table[:].indirect(two_t[:]))
-        two_words = keep.tile([P, S], U32, name="two_words", align_bytes=64)
-        nc.vector.tensor_copy(two_words[:], x_table[:].indirect(two_t[:]))
-
         w2_bf = keep.tile([P, N, PACK], BF16, name="w2_bf", align_bytes=64)
         interleave(nc.vector.tensor_copy, w2_bf, w2_raw)
+        two_words = keep.tile([P, S], U32, name="two_words", align_bytes=64)
+        nc.vector.tensor_copy(two_words[:], x_table[:].indirect(two_t[:]))
         w1_raw = keep.tile([P, PACK, N], F32, name="w1_raw", tag="w_raw")
-        nc.sync.dma_start(w1_raw[:], w1.rearrange("(p j) n -> p j n", j=PACK))
+        w1_rows = w1.rearrange("(b t r) n -> t b r n", t=PACK, r=RUN)
+        for t in range(PACK):
+            nc.sync.dma_start(w1_raw[:, t, :], w1_rows[t])
 
         total = []
         scaled = []
         for t in range(PACK):
             twin = keep.tile([P, S], F32, name="ex_twin%d" % t)
-            nc.sync.dma_start(twin[:], ex[t][:])
+            if t == 0:
+                nc.vector.tensor_copy(twin[:], ex[t][:])
+            else:
+                nc.sync.dma_start(twin[:], ex[t][:])
             tot = keep.tile([P, S], F32, name="total%d" % t)
             for a in range(2):
                 nc.vector.tensor_tensor(tot[:, half(a)], ex[t][:].indirect(half_list(n1_t, a)), twin[:, half(a)], ALU.add)
             total.append(tot)
             sc = keep.tile([P, S], F32, name="scaled%d" % t)
-            nc.scalar.activation(sc[:], score_ps[t][:], ACT.Copy, scale=gain[:, t : t + 1])
+            nc.scalar.activation(sc[:], score_ps[t][:], ACT.Copy, scale=gain[t][:])
             scaled.append(sc)
 
         w2_codes, w2_scales = quantize(w2_bf, N, "w2")
@@ -146,7 +156,6 @@ def tile_picked_kmixlsehop_none_p_kernel(tc, x_words, x_scales, d_words, d_scale
         w1_codes, w1_scales = quantize(w1_bf, N, "w1")
 
         h_ps = {}
-        h = [keep.tile([P, S], F32, name="h%d" % m) for m in range(PACK)]
         for a in range(2):
             z_planes = keep.tile([P, PACK, HALF], BF16, name="z_planes%d" % a)
             for t in range(PACK):
@@ -154,7 +163,7 @@ def tile_picked_kmixlsehop_none_p_kernel(tc, x_words, x_scales, d_words, d_scale
                 nc.scalar.activation(picked[:], scaled[t][:].indirect(half_list(n2_t, a)), ACT.Copy, scale=-0.0625)
                 lse = keep.tile([P, HALF], F32, name="lse%d_%d" % (a, t))
                 nc.scalar.activation(lse[:], total[t][:, half(a)], ACT.Ln)
-                nc.vector.scalar_tensor_tensor(z_planes[:, t, :], lse[:], gain[:, t : t + 1], picked[:], ALU.mult, ALU.add)
+                nc.vector.scalar_tensor_tensor(z_planes[:, t, :], lse[:], gain[t][:], picked[:], ALU.mult, ALU.add)
             z_bf = keep.tile([P, HALF, PACK], BF16, name="z_bf%d" % a, align_bytes=64)
             interleave(nc.vector.tensor_copy, z_bf, z_planes)
             z_codes, z_scales = quantize(z_bf, HALF, "z%d" % a)
@@ -180,27 +189,24 @@ def tile_picked_kmixlsehop_none_p_kernel(tc, x_words, x_scales, d_words, d_scale
                     stop=True,
                 )
                 h_ps[a, m] = ps
-                if a == 0:
-                    nc.scalar.copy(h[m][:, half(a)], ps[:])
+
+        h = [keep.tile([P, S], F32, name="h%d" % m) for m in range(PACK)]
+        h_halved = [keep.tile([P, S], F32, name="h_halved%d" % m) for m in range(PACK)]
+        for a in range(2):
+            for m in range(PACK):
+                nc.scalar.activation(h_halved[m][:, half(a)], h_ps[a, m][:], ACT.Copy, scale=0.5)
+                nc.scalar.copy(h[m][:, half(a)], h_ps[a, m][:])
+
+        st = [keep.tile([P, S], F32, name="st%d" % m) for m in range(PACK)]
+        for m in range(PACK):
+            for a in range(2):
+                nc.vector.tensor_tensor(st[m][:, half(a)], h_halved[m][:].indirect(half_list(n3_t, a)), h[m][:, half(a)], ALU.add)
 
         for m in range(PACK):
-            nc.scalar.copy(h[m][:, half(1)], h_ps[1, m][:])
-            neg_st = keep.tile([P, S], F32, name="neg_st%d" % m)
-            for a in (1, 0):
-                hop = keep.tile([P, HALF], F32, name="hop%d_%d" % (m, a))
-                if m == 0 and a == 1:
-                    nc.vector.tensor_copy(hop[:], h[m][:].indirect(half_list(n3_t, a)))
-                    nc.vector.scalar_tensor_tensor(neg_st[:, half(a)], hop[:], -0.5, h[m][:, half(a)], ALU.mult, ALU.subtract)
-                else:
-                    nc.scalar.activation(hop[:], h[m][:].indirect(half_list(n3_t, a)), ACT.Copy, scale=-0.5)
-                    nc.vector.tensor_tensor(neg_st[:, half(a)], hop[:], h[m][:, half(a)], ALU.subtract)
+            other = keep.tile([P, S], F32, name="other%d" % m)
             res = keep.tile([P, S], F32, name="res%d" % m)
             for a in range(2):
-                other = keep.tile([P, HALF], F32, name="other%d_%d" % (m, a))
-                if a == 0 or m == 0:
-                    nc.vector.tensor_copy(other[:], neg_st[:, half(a)])
-                    nc.vector.tensor_tensor(res[:, half(a)], neg_st[:].indirect(half_list(n4_t, a)), other[:], ALU.subtract)
-                else:
-                    nc.scalar.activation(other[:], neg_st[:].indirect(half_list(n4_t, a)), ACT.Copy)
-                    nc.vector.tensor_tensor(res[:, half(a)], other[:], neg_st[:, half(a)], ALU.subtract)
-            nc.sync.dma_start(out[m * P : (m + 1) * P, :], res[:])
+                nc.scalar.activation(other[:, half(a)], st[m][:].indirect(half_list(n4_t, a)), ACT.Copy)
+            for cols in [slice(0, S)] if m < PACK - 1 else [half(0), half(1)]:
+                nc.vector.tensor_tensor(res[:, cols], st[m][:, cols], other[:, cols], ALU.subtract)
+                nc.sync.dma_start(out[m * P : (m + 1) * P, cols], res[:, cols])

from contextlib import ExitStack

import concourse.mybir as mybir

K, T, S, N, G, H = 512, 2048, 512, 512, 2048, 512
FLOPS = 3 * 2 * 512 * 512 * 512

F32 = mybir.dt.float32
BF16 = mybir.dt.bfloat16
I32 = mybir.dt.int32
U32 = mybir.dt.uint32
U16 = mybir.dt.uint16
U8 = mybir.dt.uint8
FP8X4 = mybir.dt.float8_e4m3fn_x4
ACT = mybir.ActivationFunctionType
ALU = mybir.AluOpType

P = 128
PACK = 4
RUN = 8
HALF = S // 2
HALF_COLS = HALF // 16


def tile_picked_kmixlsehop_none_p_kernel(tc, x_words, x_scales, d_words, d_scales, gn, w1, w2, offs, k1, n1, n2, two, n3, n4, out):
    nc = tc.nc
    with ExitStack() as ctx:
        lists = ctx.enter_context(tc.tile_pool(name="lists", bufs=1))
        keep = ctx.enter_context(tc.tile_pool(name="keep", bufs=1))
        psum = ctx.enter_context(tc.psum_pool(name="psum", bufs=1))

        def load_list(src, name):
            t = lists.tile([P, S // 16], U16, name=name)
            nc.sync.dma_start(t[:], src)
            return t

        def half(a):
            return slice(a * HALF, (a + 1) * HALF)

        def half_list(lst, a):
            return lst[:, a * HALF_COLS : (a + 1) * HALF_COLS]

        d_scale_table = keep.tile([P, G], U8, name="d_scale_table", align_bytes=64)
        x_scale_table = keep.tile([P, T], U8, name="x_scale_table", align_bytes=64)
        nc.vector.memset(x_scale_table[:].bitcast(I32), 0)
        gain = [keep.tile([P, 1], F32, name="gain%d" % t) for t in range(PACK)]
        gain_rows = gn.rearrange("(b t r) o -> t b r o", t=PACK, r=RUN)
        for t in range(PACK):
            nc.gpsimd.dma_start(gain[t][:], gain_rows[t])

        k1_t = load_list(k1, "k1_t")
        nc.sync.dma_start(
            d_scale_table[:].bitcast(I32),
            d_scales[0].bitcast(I32).unsqueeze(1).to_broadcast([16, 8, G // 4]),
        )
        offs_t = load_list(offs, "offs_t")
        x_rows = x_scales[0].bitcast(I32).rearrange("(q r) c -> r q c", r=4)
        for r in range(4):
            nc.scalar.dma_start(x_scale_table[r:P:32, :].bitcast(I32), x_rows[r])
        d_table = keep.tile([P, G], U32, name="d_table", align_bytes=64)
        nc.sync.dma_start(d_table[:].bitcast(I32), d_words[0].rearrange("p n t -> p (n t)").bitcast(I32))
        x_table = keep.tile([P, T], U32, name="x_table", align_bytes=64)
        nc.sync.dma_start(x_table[:].bitcast(I32), x_words[0].rearrange("p n t -> p (n t)").bitcast(I32))
        two_t = load_list(two, "two_t")
        n1_t = load_list(n1, "n1_t")
        n2_t = load_list(n2, "n2_t")
        w2_raw = keep.tile([P, PACK, N], F32, name="w2_raw", tag="w_raw")
        nc.sync.dma_start(w2_raw[:], w2.rearrange("(p j) n -> p j n", j=PACK))
        n3_t = load_list(n3, "n3_t")
        n4_t = load_list(n4, "n4_t")

        key_scales_picked = keep.tile([P, H], U8, name="key_scales_picked", align_bytes=64)
        nc.vector.tensor_copy(key_scales_picked[:], d_scale_table[:].indirect(k1_t[:]))
        key_scales = keep.tile([P, H], U8, name="key_scales", align_bytes=64)
        nc.vector.tensor_copy(
            key_scales[:].bitcast(I32).rearrange("p (t b r) -> p t b r", t=PACK, r=RUN // 4),
            key_scales_picked[:].bitcast(I32).rearrange("p (b t r) -> p t b r", t=PACK, r=RUN // 4),
        )
        for r in range(1, 4):
            nc.scalar.dma_start(key_scales[r:P:32, :].bitcast(I32), key_scales[8 * r : P : 32, :].bitcast(I32))

        def interleave(eng_copy, dst, src):
            eng_copy(
                dst[:].rearrange("p (c i) t -> p c t i", i=4),
                src[:].rearrange("p t (c i) -> p c t i", i=4),
            )

        def quantize(src, width, name):
            codes = keep.tile([P, width], U32, name=name + "_codes", align_bytes=64)
            scales = keep.tile([P, width], U8, name=name + "_scales", align_bytes=64)
            nc.vector.quantize_mx(out=codes[:].bitcast(FP8X4), scales=scales[:], in_=src[:].rearrange("p n t -> p (n t)"))
            return codes, scales

        key_words_picked = keep.tile([P, H], U32, name="key_words_picked", align_bytes=64)
        nc.vector.tensor_copy(key_words_picked[:], d_table[:].indirect(k1_t[:]))
        key_words = keep.tile([P, H], U32, name="key_words", align_bytes=64)
        nc.vector.tensor_copy(
            key_words[:].rearrange("p (t b r) -> p t b r", t=PACK, r=RUN),
            key_words_picked[:].rearrange("p (b t r) -> p t b r", t=PACK, r=RUN),
        )
        q_scales = keep.tile([P, S], U8, name="q_scales", align_bytes=64)
        nc.vector.tensor_copy(q_scales[:], x_scale_table[:].indirect(offs_t[:]))
        q_words = keep.tile([P, S], U32, name="q_words", align_bytes=64)
        nc.vector.tensor_copy(q_words[:], x_table[:].indirect(offs_t[:]))

        score_ps = []
        for t in range(PACK):
            ps = psum.tile([P, S], F32, name="score%d" % t, tag="bank%d" % t)
            nc.tensor.matmul_mx(
                out=ps[:],
                lhsT=key_words[:, t * P : (t + 1) * P].bitcast(FP8X4),
                lhsT_scale=key_scales[:, t * P : (t + 1) * P],
                rhs=q_words[:].bitcast(FP8X4),
                rhs_scale=q_scales[:],
                start=True,
                stop=True,
            )
            score_ps.append(ps)

        ex = []
        for t in range(PACK):
            e = keep.tile([P, S], F32, name="ex%d" % t)
            nc.scalar.activation(e[:], score_ps[t][:], ACT.Exp, scale=0.0625)
            ex.append(e)

        two_scales = keep.tile([P, S], U8, name="two_scales", align_bytes=64)
        nc.vector.tensor_copy(two_scales[:], x_scale_table[:].indirect(two_t[:]))
        w2_bf = keep.tile([P, N, PACK], BF16, name="w2_bf", align_bytes=64)
        interleave(nc.vector.tensor_copy, w2_bf, w2_raw)
        two_words = keep.tile([P, S], U32, name="two_words", align_bytes=64)
        nc.vector.tensor_copy(two_words[:], x_table[:].indirect(two_t[:]))
        w1_raw = keep.tile([P, PACK, N], F32, name="w1_raw", tag="w_raw")
        w1_rows = w1.rearrange("(b t r) n -> t b r n", t=PACK, r=RUN)
        for t in range(PACK):
            nc.sync.dma_start(w1_raw[:, t, :], w1_rows[t])

        total = []
        scaled = []
        for t in range(PACK):
            twin = keep.tile([P, S], F32, name="ex_twin%d" % t)
            if t == 0:
                nc.vector.tensor_copy(twin[:], ex[t][:])
            else:
                nc.sync.dma_start(twin[:], ex[t][:])
            tot = keep.tile([P, S], F32, name="total%d" % t)
            for a in range(2):
                nc.vector.tensor_tensor(tot[:, half(a)], ex[t][:].indirect(half_list(n1_t, a)), twin[:, half(a)], ALU.add)
            total.append(tot)
            sc = keep.tile([P, S], F32, name="scaled%d" % t)
            nc.scalar.activation(sc[:], score_ps[t][:], ACT.Copy, scale=gain[t][:])
            scaled.append(sc)

        w2_codes, w2_scales = quantize(w2_bf, N, "w2")
        w1_bf = keep.tile([P, N, PACK], BF16, name="w1_bf", align_bytes=64)
        interleave(nc.vector.tensor_copy, w1_bf, w1_raw)
        w1_codes, w1_scales = quantize(w1_bf, N, "w1")

        h_ps = {}
        for a in range(2):
            z_planes = keep.tile([P, PACK, HALF], BF16, name="z_planes%d" % a)
            for t in range(PACK):
                picked = keep.tile([P, HALF], F32, name="picked%d_%d" % (a, t))
                nc.scalar.activation(picked[:], scaled[t][:].indirect(half_list(n2_t, a)), ACT.Copy, scale=-0.0625)
                lse = keep.tile([P, HALF], F32, name="lse%d_%d" % (a, t))
                nc.scalar.activation(lse[:], total[t][:, half(a)], ACT.Ln)
                nc.vector.scalar_tensor_tensor(z_planes[:, t, :], lse[:], gain[t][:], picked[:], ALU.mult, ALU.add)
            z_bf = keep.tile([P, HALF, PACK], BF16, name="z_bf%d" % a, align_bytes=64)
            interleave(nc.vector.tensor_copy, z_bf, z_planes)
            z_codes, z_scales = quantize(z_bf, HALF, "z%d" % a)
            for m in range(PACK):
                ps = psum.tile([P, HALF], F32, name="h_ps%d_%d" % (a, m), tag="bank%d" % (PACK * (1 - a) + m))
                cols = slice(m * P, (m + 1) * P)
                nc.tensor.matmul_mx(
                    out=ps[:],
                    lhsT=w2_codes[:, cols].bitcast(FP8X4),
                    lhsT_scale=w2_scales[:, cols],
                    rhs=two_words[:, half(a)].bitcast(FP8X4),
                    rhs_scale=two_scales[:, half(a)],
                    start=True,
                    stop=False,
                )
                nc.tensor.matmul_mx(
                    out=ps[:],
                    lhsT=w1_codes[:, cols].bitcast(FP8X4),
                    lhsT_scale=w1_scales[:, cols],
                    rhs=z_codes[:].bitcast(FP8X4),
                    rhs_scale=z_scales[:],
                    start=False,
                    stop=True,
                )
                h_ps[a, m] = ps

        h = [keep.tile([P, S], F32, name="h%d" % m) for m in range(PACK)]
        h_halved = [keep.tile([P, S], F32, name="h_halved%d" % m) for m in range(PACK)]
        for a in range(2):
            for m in range(PACK):
                nc.scalar.activation(h_halved[m][:, half(a)], h_ps[a, m][:], ACT.Copy, scale=0.5)
                nc.scalar.copy(h[m][:, half(a)], h_ps[a, m][:])

        st = [keep.tile([P, S], F32, name="st%d" % m) for m in range(PACK)]
        for m in range(PACK):
            for a in range(2):
                nc.vector.tensor_tensor(st[m][:, half(a)], h_halved[m][:].indirect(half_list(n3_t, a)), h[m][:, half(a)], ALU.add)

        for m in range(PACK):
            other = keep.tile([P, S], F32, name="other%d" % m)
            res = keep.tile([P, S], F32, name="res%d" % m)
            for a in range(2):
                nc.scalar.activation(other[:, half(a)], st[m][:].indirect(half_list(n4_t, a)), ACT.Copy)
            for cols in [slice(0, S)] if m < PACK - 1 else [half(0), half(1)]:
                nc.vector.tensor_tensor(res[:, cols], st[m][:, cols], other[:, cols], ALU.subtract)
                nc.sync.dma_start(out[m * P : (m + 1) * P, cols], res[:, cols])
